import numpy as np
import ml_dtypes


def mxq(x, axis, fmt="e4m3"):
    dtype, down = {"e4m3": (ml_dtypes.float8_e4m3fn, 7), "e5m2": (ml_dtypes.float8_e5m2, 14)}[fmt]
    v = np.moveaxis(np.asarray(x, np.float32).astype(ml_dtypes.bfloat16).astype(np.float64), axis, -1)
    blocks = v.reshape(v.shape[:-1] + (-1, 32))
    amax = np.abs(blocks).max(-1, keepdims=True)
    byte = np.maximum(np.where(amax > 0, np.frexp(amax)[1] - 1 + 127, 0) - down, 1)
    scale = np.exp2(byte - 127.0)
    codes = (blocks / scale).astype(np.float32).astype(dtype).astype(np.float64)
    return np.moveaxis((codes * scale).reshape(v.shape), -1, axis)


WIDE = False


def mx_kscale(k):
    if not WIDE:
        return np.ones(k)
    levels = np.array([10, -10, 5, -5, 0])
    if k % 512:
        return np.exp2(np.random.permutation(np.resize(levels, k // 32))).repeat(32)
    a = np.empty((k // 512, 16))
    for p in range(k // 512):
        a[p, :8] = np.random.permutation(np.resize(levels, 8))
        for g in range(8):
            far = levels[np.abs(levels - a[p, g]) >= 10]
            a[p, g + 8] = far[np.random.randint(len(far))]
    return np.exp2(a.ravel()).repeat(32)


def f64(x):
    return np.asarray(x).astype(np.float64)


def striped(idx):
    return np.tile(np.asarray(idx).reshape(-1, 16).T, (8, 1)).astype(np.uint16)


def unstriped(offs):
    return offs[:16].T.reshape(-1).astype(np.int64)


E2M1 = np.array([0.0, 0.5, 1.0, 1.5, 2.0, 3.0, 4.0, 6.0, -0.0, -0.5, -1.0, -1.5, -2.0, -3.0, -4.0, -6.0])


def pack_weight(w, fmt):
    k, n = w.shape
    w = f64(np.asarray(w, np.float32).astype(ml_dtypes.bfloat16)).reshape(k // 32, 32, n)
    amax = np.abs(w).max(1)
    if fmt == "e4m3":
        byte = np.frexp(amax)[1] - 1 + 127 - 7
    else:
        mant, ex = np.frexp(amax / 6.0)
        byte = np.where(mant > 0.5, ex, ex - 1) + 127
    byte = np.clip(np.where(amax > 0, byte, 1), 1, 254)
    scaled = (w * np.exp2(127.0 - byte)[:, None, :]).reshape(k, n).astype(np.float32)
    by_word = np.ascontiguousarray(scaled.reshape(k // 512, 128, 4, n).transpose(0, 1, 3, 2))
    if fmt == "e4m3":
        words = by_word.astype(ml_dtypes.float8_e4m3fn).view(np.uint8)
    else:
        c = by_word.astype(ml_dtypes.float4_e2m1fn).view(np.uint8) & 0xF
        words = (c[..., 0::2] | (c[..., 1::2] << 4)).reshape(k // 512, 128, 2 * n)
    return np.ascontiguousarray(words), np.ascontiguousarray(byte.astype(np.uint8).reshape(k // 512, 16, n))


def unpack_weight(words, scales, fmt):
    g, _, n = scales.shape
    words = np.ascontiguousarray(words).reshape(g, 128, n, -1)
    if fmt == "e4m3":
        vals = words.view(ml_dtypes.float8_e4m3fn).astype(np.float64)
    else:
        nib = np.empty((g, 128, n, 4), np.uint8)
        nib[..., 0::2] = words & 0xF
        nib[..., 1::2] = words >> 4
        vals = E2M1[nib]
    vals = vals * np.repeat(np.exp2(scales.astype(np.float64) - 127.0), 8, axis=1)[..., None]
    return vals.transpose(0, 1, 3, 2).reshape(g * 512, n)


def sigmoid(v):
    return 1.0 / (1.0 + np.exp(-v))


D, E, T, I, Q = 512, 512, 2048, 512, 128


def setup_inputs():
    n = np.random.standard_normal
    idx = np.random.permutation(T)[:I]
    fd = mx_kscale(D)
    fe = mx_kscale(E)
    keysp = pack_weight(n((D, T)) / fd[:, None], "e2m1")
    valsp = pack_weight(n((E, T)) / fe[:, None], "e2m1")
    return {
        "query": (n((D, Q)) * 1.0 / np.sqrt(D) * fd[:, None]).astype(np.float32),
        "query2": (n((D, Q)) * 1.0 / np.sqrt(D) * fd[:, None]).astype(np.float32),
        "keys_words": keysp[0],
        "keys_scales": keysp[1],
        "th": (np.random.uniform(0.3, 1.5, (Q, 1))).astype(np.float32),
        "gout": (n((E, Q)) * 1 / np.sqrt(E) * fe[:, None]).astype(np.float32),
        "vals_words": valsp[0],
        "vals_scales": valsp[1],
        "size": (np.random.uniform(0.5, 2.0, (1, I))).astype(np.float32),
        "base": (0.5 * n((Q, T))).astype(np.float32),
        "gq1": (np.random.uniform(0.3, 1.5, (Q, 1))).astype(np.float32),
        "offs": striped(idx),
    }


def reference(query, query2, keys_words, keys_scales, th, gout, vals_words, vals_scales, size, base, gq1, offs):
    idx = unstriped(offs)
    keysu = unpack_weight(keys_words, keys_scales, "e2m1")
    valsu = unpack_weight(vals_words, vals_scales, "e2m1")
    queryq = mxq(f64(query), 0, "e4m3")
    keysidxg = keysu[:, idx]
    a = queryq.T @ keysidxg
    query2q = mxq(f64(query2), 0, "e4m3")
    b = query2q.T @ keysidxg
    ua = sigmoid(a - f64(th))
    ub = sigmoid(b - f64(th))
    p = 1.0 - (1.0 - ua) * (1.0 - ub)
    z = np.sum(p, axis=1, keepdims=True)
    goutq = mxq(f64(gout), 0, "e4m3")
    valsidxg = valsu[:, idx]
    c0 = goutq.T @ valsidxg
    dz = np.sum(c0 * p * f64(size) / np.square(z) * (-1.0), axis=1, keepdims=True)
    dp = c0 / z * f64(size) + dz
    dua = dp * (-1.0) * (1.0 - ub) * (-1.0)
    da = dua * ua * (1.0 - ua)
    hda = da * 512.0 * 2.0 * 512.0
    hdua = hda * (1.0 - ua) * ua
    hdp = hdua * (-1.0) * (1.0 - ub) * (-1.0)
    hdz = np.sum(hdp, axis=1, keepdims=True)
    hz = np.sum(hdp * f64(size) * c0 / np.square(z) * (-1.0), axis=1, keepdims=True) + np.sum(hdz * (-1.0) * c0 * p * f64(size) / np.square(np.square(z)) * (-1.0), axis=1, keepdims=True) * z * 2.0
    hp = hdz * (-1.0) / np.square(z) * c0 * f64(size) + hz
    hua = hda * (1.0 - ua) * dua - hda * dua * ua - hp * (-1.0) * (1.0 - ub)
    ha = hua * ua * (1.0 - ua)
    gs = ha * f64(gq1)
    gf = np.zeros((Q, T))
    gf[:, idx] = gs
    y = f64(base) + gf
    return y

@@ -1,0 +1,176 @@
+from contextlib import ExitStack
+
+import concourse.mybir as mybir
+
+F32 = mybir.dt.float32
+BF16 = mybir.dt.bfloat16
+I32 = mybir.dt.int32
+U32 = mybir.dt.uint32
+U16 = mybir.dt.uint16
+U8 = mybir.dt.uint8
+FP8X4 = mybir.dt.float8_e4m3fn_x4
+FP4X4 = mybir.dt.float4_e2m1fn_x4
+ALU = mybir.AluOpType
+ACT = mybir.ActivationFunctionType
+
+P = 128
+PACK = 4
+TOKENS = 2048
+SLOTS = 512
+ROWS = 128
+PENALTY = 2.0 * 512.0 * 512.0
+STORE_WIDTHS = (256, 512, 512, 512, 256)
+
+FLOPS = 3 * 2 * 512 * ROWS * SLOTS
+
+
+def tile_attend_gpeitherquestion_kernel(tc, query, query2, keys_words, keys_scales, th, gout, vals_words,
+                                         vals_scales, size, base, gq1, offs, out):
+    nc = tc.nc
+    with ExitStack() as ctx:
+        pool = ctx.enter_context(tc.tile_pool(name="held", bufs=1))
+        psum = ctx.enter_context(tc.psum_pool(name="psum", bufs=1))
+
+        def wide(name):
+            return pool.tile([P, SLOTS], F32, name=name)
+
+        def column(name):
+            return pool.tile([P, 1], F32, name=name)
+
+        offsets = pool.tile([P, SLOTS // 16], U16, name="offsets")
+        nc.sync.dma_start(offsets[:], offs)
+
+        def load_scale_rows(scales, name):
+            plane = pool.tile([P, TOKENS], U8, name=name, tag=name)
+            nc.vector.memset(plane[:].bitcast(I32), 0)
+            for quad in range(4):
+                nc.sync.dma_start(plane[32 * quad:32 * quad + 4, :].bitcast(I32),
+                                  scales[0, 4 * quad:4 * quad + 4, :].bitcast(I32))
+            return plane
+
+        def load_words(words, name):
+            table = pool.tile([P, TOKENS], U16, name=name, tag=name)
+            nc.sync.dma_start(table[:].bitcast(I32), words[0].bitcast(I32))
+            return table
+
+        def load_rows(queue, rows, name, tag):
+            raw = pool.tile([P, PACK, ROWS], F32, name=name, tag=tag, align_bytes=64)
+            queue.dma_start(raw[:], rows.rearrange("(p t) q -> p t q", t=PACK))
+            return raw
+
+        key_plane = load_scale_rows(keys_scales, "key_plane")
+        key_table = load_words(keys_words, "key_table")
+        raw_b = load_rows(nc.sync, query2, "raw_b", "stage0")
+        raw_a = load_rows(nc.sync, query, "raw_a", "stage1")
+        val_table = load_words(vals_words, "val_table")
+        val_plane = load_scale_rows(vals_scales, "val_plane")
+        raw_c = load_rows(nc.sync, gout, "raw_c", "stage2")
+
+        th_sb = column("th_sb")
+        nc.gpsimd.dma_start(th_sb[:], th)
+        gq_sb = column("gq_sb")
+        nc.gpsimd.dma_start(gq_sb[:], gq1)
+
+        placed = pool.tile([P, TOKENS], F32, name="placed")
+        nc.vector.memset(placed[:], 0.0)
+
+        half_th = column("half_th")
+        nc.gpsimd.tensor_scalar(half_th[:], th_sb[:], 0.5, 0.0, ALU.mult, ALU.add)
+
+        def interleave(raw, name):
+            grouped = pool.tile([P, ROWS, PACK], BF16, name=name, align_bytes=64)
+            nc.scalar.activation(grouped[:], raw[:].rearrange("p t q -> p q t"), ACT.Copy)
+            return grouped
+
+        def quantize(grouped, name):
+            codes = pool.tile([P, ROWS], U32, name=name + "_codes", align_bytes=64)
+            plane = pool.tile([P, ROWS], U8, name=name + "_plane", align_bytes=64)
+            nc.vector.quantize_mx(out=codes[:].bitcast(FP8X4), scales=plane[:],
+                                  in_=grouped[:].rearrange("p q t -> p (q t)"))
+            return codes, plane
+
+        def gather(table, dtype, name, tag):
+            picked = pool.tile([P, SLOTS], dtype, name=name, tag=tag, align_bytes=64)
+            nc.vector.tensor_copy(picked[:], table[:].indirect(offsets[:]))
+            return picked
+
+        def product(stationary, words, plane, name):
+            bank = psum.tile([P, SLOTS], F32, name=name)
+            nc.tensor.matmul_mx(out=bank[:], lhsT=stationary[0][:].bitcast(FP8X4), lhsT_scale=stationary[1][:],
+                                rhs=words[:].bitcast(FP4X4), rhs_scale=plane[:], start=True, stop=True)
+            return bank
+
+        grouped_b = interleave(raw_b, "grouped_b")
+        grouped_a = interleave(raw_a, "grouped_a")
+        size_row = wide("size_row")
+        nc.sync.dma_start(size_row[:], size[0].partition_broadcast(P))
+        key_words = gather(key_table, U16, "key_words", "key_words")
+        key_bytes = gather(key_plane, U8, "key_bytes", "key_bytes")
+        quant_b = quantize(grouped_b, "qb")
+        quant_a = quantize(grouped_a, "qa")
+        score_b = product(quant_b, key_words, key_bytes, "score_b")
+        score_a = product(quant_a, key_words, key_bytes, "score_a")
+
+        grouped_c = interleave(raw_c, "grouped_c")
+        val_words = gather(val_table, U16, "val_words", "stage1")
+        base_sb = pool.tile([P, TOKENS], F32, name="base_sb")
+        nc.sync.dma_start(base_sb[:], base)
+        val_bytes = gather(val_plane, U8, "val_bytes", "val_bytes")
+        quant_c = quantize(grouped_c, "qc")
+        c0 = product(quant_c, val_words, val_bytes, "c0")
+
+        gq_k = column("gq_k")
+        nc.gpsimd.tensor_scalar(gq_k[:], gq_sb[:], PENALTY / 16.0, 0.0, ALU.mult, ALU.add)
+
+        tb = pool.tile([P, SLOTS], F32, name="tb", tag="stage2", align_bytes=64)
+        nc.scalar.activation(tb[:], score_b[:], ACT.Tanh, bias=half_th[:], scale=-0.5)
+        u = wide("u")
+        nc.scalar.activation(u[:], score_a[:], ACT.Tanh, bias=half_th[:], scale=-0.5)
+        v = wide("v")
+        nc.scalar.activation(v[:], tb[:], ACT.Copy, bias=0.5, scale=0.5)
+
+        m2 = pool.tile([P, SLOTS], F32, name="m2", tag="val_plane")
+        nc.vector.scalar_tensor_tensor(m2[:], u[:], 1.0, v[:], ALU.add, ALU.mult)
+        p = wide("p")
+        z = column("z")
+        nc.scalar.activation(p[:], m2[:], ACT.Copy, bias=1.0, scale=-0.5, accum_out=z[:])
+        g = wide("g")
+        nc.vector.scalar_tensor_tensor(g[:], u[:], 1.0, m2[:], ALU.subtract, ALU.mult)
+        cs = wide("cs")
+        nc.vector.tensor_tensor(cs[:], c0[:], size_row[:], ALU.mult)
+        r = column("r")
+        nc.vector.reciprocal(r[:], z[:])
+        weighted = wide("weighted")
+        mean = column("mean")
+        nc.vector.scalar_tensor_tensor(weighted[:], cs[:], r[:], p[:], ALU.mult, ALU.mult, accum_out=mean[:])
+        kappa = column("kappa")
+        nc.vector.tensor_scalar(kappa[:], r[:], r[:], gq_k[:], ALU.mult, ALU.mult)
+        lam = column("lam")
+        nc.vector.tensor_scalar(lam[:], kappa[:], r[:], 0.25, ALU.mult, ALU.mult)
+        g_lam = wide("g_lam")
+        nc.scalar.activation(g_lam[:], g[:], ACT.Copy, scale=lam[:])
+        f = wide("f")
+        nc.vector.scalar_tensor_tensor(f[:], cs[:], mean[:], g[:], ALU.subtract, ALU.mult)
+        f_sq = wide("f_sq")
+        sum_ff = column("sum_ff")
+        nc.scalar.activation(f_sq[:], f[:], ACT.Square, accum_out=sum_ff[:])
+        fg = wide("fg")
+        alpha = column("alpha")
+        nc.vector.scalar_tensor_tensor(fg[:], f[:], lam[:], g[:], ALU.mult, ALU.mult, accum_out=alpha[:])
+        curve = wide("curve")
+        nc.vector.scalar_tensor_tensor(curve[:], f[:], kappa[:], u[:], ALU.mult, ALU.mult)
+        term_g = wide("term_g")
+        nc.scalar.activation(term_g[:], g_lam[:], ACT.Copy, scale=sum_ff[:])
+        term_f = wide("term_f")
+        nc.vector.scalar_tensor_tensor(term_f[:], curve[:], alpha[:], f[:], ALU.add, ALU.mult)
+
+        nc.vector.tensor_tensor(placed[:].indirect(offsets[:]), term_f[:], term_g[:], ALU.add)
+
+        start = 0
+        for n, width in enumerate(STORE_WIDTHS):
+            cols = slice(start, start + width)
+            result = pool.tile([P, width], F32, name="result%d" % n)
+            nc.vector.tensor_tensor(result[:], placed[:, cols], base_sb[:, cols], ALU.add)
+            queue = nc.sync if n % 2 == 0 else nc.scalar
+            queue.dma_start(out[:, cols], result[:])
+            start = start + width

@@ -1,6 +1,7 @@
 from contextlib import ExitStack
 
 import concourse.mybir as mybir
+from concourse.masks import make_identity
 
 F32 = mybir.dt.float32
 BF16 = mybir.dt.bfloat16
@@ -39,46 +40,59 @@ def tile_attend_gpeitherquestion_kernel(tc, query, query2, keys_words, keys_scal
 
         offsets = pool.tile([P, SLOTS // 16], U16, name="offsets")
         nc.sync.dma_start(offsets[:], offs)
+        size4 = pool.tile([P, PACK], F32, name="size4")
+        nc.sync.dma_start(size4[:], size.rearrange("o (p c) -> (o p) c", c=PACK))
+        th_sb = column("th_sb")
+        nc.sync.dma_start(th_sb[:], th)
+        gq_sb = column("gq_sb")
+        nc.sync.dma_start(gq_sb[:], gq1)
 
         def load_scale_rows(scales, name):
-            plane = pool.tile([P, TOKENS], U8, name=name, tag=name)
-            nc.vector.memset(plane[:].bitcast(I32), 0)
-            for quad in range(4):
-                nc.sync.dma_start(plane[32 * quad:32 * quad + 4, :].bitcast(I32),
-                                  scales[0, 4 * quad:4 * quad + 4, :].bitcast(I32))
-            return plane
+            rows = pool.tile([P, TOKENS], U8, name=name)
+            nc.vector.memset(rows[:, :TOKENS // 2].bitcast(I32), 0)
+            nc.gpsimd.memset(rows[:, TOKENS // 2:].bitcast(I32), 0)
+            nc.sync.dma_start(rows[0:P:8, :].bitcast(I32), scales[0].bitcast(I32))
+            return rows
 
         def load_words(words, name):
             table = pool.tile([P, TOKENS], U16, name=name, tag=name)
             nc.sync.dma_start(table[:].bitcast(I32), words[0].bitcast(I32))
             return table
 
-        def load_rows(queue, rows, name, tag):
+        def load_rows(rows, name, tag):
             raw = pool.tile([P, PACK, ROWS], F32, name=name, tag=tag, align_bytes=64)
-            queue.dma_start(raw[:], rows.rearrange("(p t) q -> p t q", t=PACK))
+            nc.sync.dma_start(raw[:], rows.rearrange("(p t) q -> p t q", t=PACK))
             return raw
 
-        key_plane = load_scale_rows(keys_scales, "key_plane")
+        key_rows = load_scale_rows(keys_scales, "key_rows")
+        val_rows = load_scale_rows(vals_scales, "val_rows")
         key_table = load_words(keys_words, "key_table")
-        raw_b = load_rows(nc.sync, query2, "raw_b", "stage0")
-        raw_a = load_rows(nc.sync, query, "raw_a", "stage1")
+        raw_b = load_rows(query2, "raw_b", "raw_b")
+        raw_a = load_rows(query, "raw_a", "stage")
         val_table = load_words(vals_words, "val_table")
-        val_plane = load_scale_rows(vals_scales, "val_plane")
-        raw_c = load_rows(nc.sync, gout, "raw_c", "stage2")
+        raw_c = load_rows(gout, "raw_c", "raw_c")
 
-        th_sb = column("th_sb")
-        nc.gpsimd.dma_start(th_sb[:], th)
-        gq_sb = column("gq_sb")
-        nc.gpsimd.dma_start(gq_sb[:], gq1)
+        def zeroed_plane(name):
+            plane = pool.tile([P, SLOTS], U8, name=name, align_bytes=64)
+            nc.vector.memset(plane[:].bitcast(I32), 0)
+            return plane
 
-        placed = pool.tile([P, TOKENS], F32, name="placed")
-        nc.vector.memset(placed[:], 0.0)
+        key_plane = zeroed_plane("key_plane")
+        val_plane = zeroed_plane("val_plane")
 
+        identity = pool.tile([P, P], F32, name="identity")
+        make_identity(nc, identity[:])
         half_th = column("half_th")
-        nc.gpsimd.tensor_scalar(half_th[:], th_sb[:], 0.5, 0.0, ALU.mult, ALU.add)
+        nc.scalar.activation(half_th[:], th_sb[:], ACT.Copy, scale=0.5)
+        gq_k = column("gq_k")
+        nc.scalar.activation(gq_k[:], gq_sb[:], ACT.Copy, scale=PENALTY / 16.0)
+
+        size_bank = psum.tile([P, PACK, P], F32, name="size_bank")
+        for c in range(PACK):
+            nc.tensor.transpose(size_bank[:, c, :], size4[:, c:c + 1].to_broadcast([P, P]), identity[:])
 
         def interleave(raw, name):
-            grouped = pool.tile([P, ROWS, PACK], BF16, name=name, align_bytes=64)
+            grouped = pool.tile([P, ROWS, PACK], BF16, name=name, tag=name, align_bytes=64)
             nc.scalar.activation(grouped[:], raw[:].rearrange("p t q -> p q t"), ACT.Copy)
             return grouped
 
@@ -94,48 +108,58 @@ def tile_attend_gpeitherquestion_kernel(tc, query, query2, keys_words, keys_scal
             nc.vector.tensor_copy(picked[:], table[:].indirect(offsets[:]))
             return picked
 
+        def move_rows(queue, picked, plane):
+            for j in range(4):
+                queue.dma_start(plane[j:P:32, :].bitcast(I32), picked[8 * j:P:32, :].bitcast(I32))
+
         def product(stationary, words, plane, name):
             bank = psum.tile([P, SLOTS], F32, name=name)
             nc.tensor.matmul_mx(out=bank[:], lhsT=stationary[0][:].bitcast(FP8X4), lhsT_scale=stationary[1][:],
                                 rhs=words[:].bitcast(FP4X4), rhs_scale=plane[:], start=True, stop=True)
             return bank
 
+        key_bytes = gather(key_rows, U8, "key_bytes", "key_bytes")
+        move_rows(nc.scalar, key_bytes, key_plane)
+        key_words = gather(key_table, U16, "key_words", "key_words")
         grouped_b = interleave(raw_b, "grouped_b")
         grouped_a = interleave(raw_a, "grouped_a")
-        size_row = wide("size_row")
-        nc.sync.dma_start(size_row[:], size[0].partition_broadcast(P))
-        key_words = gather(key_table, U16, "key_words", "key_words")
-        key_bytes = gather(key_plane, U8, "key_bytes", "key_bytes")
         quant_b = quantize(grouped_b, "qb")
         quant_a = quantize(grouped_a, "qa")
-        score_b = product(quant_b, key_words, key_bytes, "score_b")
-        score_a = product(quant_a, key_words, key_bytes, "score_a")
+        score_b = product(quant_b, key_words, key_plane, "score_b")
+        score_a = product(quant_a, key_words, key_plane, "score_a")
 
-        grouped_c = interleave(raw_c, "grouped_c")
-        val_words = gather(val_table, U16, "val_words", "stage1")
-        base_sb = pool.tile([P, TOKENS], F32, name="base_sb")
+        val_bytes = gather(val_rows, U8, "val_bytes", "stage")
+        move_rows(nc.sync, val_bytes, val_plane)
+        base_sb = pool.tile([P, TOKENS], F32, name="base_sb", tag="stage", align_bytes=64)
         nc.sync.dma_start(base_sb[:], base)
-        val_bytes = gather(val_plane, U8, "val_bytes", "val_bytes")
+        grouped_c = interleave(raw_c, "grouped_c")
+        val_words = gather(val_table, U16, "val_words", "val_words")
         quant_c = quantize(grouped_c, "qc")
-        c0 = product(quant_c, val_words, val_bytes, "c0")
+        placed = pool.tile([P, TOKENS], F32, name="placed", tag="grouped_c", align_bytes=64)
+        nc.gpsimd.memset(placed[:], 0.0)
+        c0 = product(quant_c, val_words, val_plane, "c0")
 
-        gq_k = column("gq_k")
-        nc.gpsimd.tensor_scalar(gq_k[:], gq_sb[:], PENALTY / 16.0, 0.0, ALU.mult, ALU.add)
+        size_row = pool.tile([P, SLOTS], F32, name="size_row", tag="grouped_b", align_bytes=64)
+        nc.scalar.activation(size_row[:].rearrange("p (n c) -> p n c", c=PACK),
+                             size_bank[:].rearrange("p c n -> p n c"), ACT.Copy)
 
-        tb = pool.tile([P, SLOTS], F32, name="tb", tag="stage2", align_bytes=64)
+        tb = wide("tb")
         nc.scalar.activation(tb[:], score_b[:], ACT.Tanh, bias=half_th[:], scale=-0.5)
         u = wide("u")
         nc.scalar.activation(u[:], score_a[:], ACT.Tanh, bias=half_th[:], scale=-0.5)
         v = wide("v")
         nc.scalar.activation(v[:], tb[:], ACT.Copy, bias=0.5, scale=0.5)
 
-        m2 = pool.tile([P, SLOTS], F32, name="m2", tag="val_plane")
-        nc.vector.scalar_tensor_tensor(m2[:], u[:], 1.0, v[:], ALU.add, ALU.mult)
+        halves = (slice(0, SLOTS // 2), slice(SLOTS // 2, SLOTS))
+        m2 = pool.tile([P, SLOTS], F32, name="m2", tag="val_table")
+        for h in halves:
+            nc.vector.scalar_tensor_tensor(m2[:, h], u[:, h], 1.0, v[:, h], ALU.add, ALU.mult)
         p = wide("p")
         z = column("z")
         nc.scalar.activation(p[:], m2[:], ACT.Copy, bias=1.0, scale=-0.5, accum_out=z[:])
         g = wide("g")
-        nc.vector.scalar_tensor_tensor(g[:], u[:], 1.0, m2[:], ALU.subtract, ALU.mult)
+        for h in halves:
+            nc.vector.scalar_tensor_tensor(g[:, h], u[:, h], 1.0, m2[:, h], ALU.subtract, ALU.mult)
         cs = wide("cs")
         nc.vector.tensor_tensor(cs[:], c0[:], size_row[:], ALU.mult)
         r = column("r")
@@ -150,19 +174,23 @@ def tile_attend_gpeitherquestion_kernel(tc, query, query2, keys_words, keys_scal
         g_lam = wide("g_lam")
         nc.scalar.activation(g_lam[:], g[:], ACT.Copy, scale=lam[:])
         f = wide("f")
-        nc.vector.scalar_tensor_tensor(f[:], cs[:], mean[:], g[:], ALU.subtract, ALU.mult)
+        for h in halves:
+            nc.vector.scalar_tensor_tensor(f[:, h], cs[:, h], mean[:], g[:, h], ALU.subtract, ALU.mult)
         f_sq = wide("f_sq")
         sum_ff = column("sum_ff")
         nc.scalar.activation(f_sq[:], f[:], ACT.Square, accum_out=sum_ff[:])
+        curve = wide("curve")
+        first, second = halves
+        nc.vector.scalar_tensor_tensor(curve[:, first], f[:, first], kappa[:], u[:, first], ALU.mult, ALU.mult)
         fg = wide("fg")
         alpha = column("alpha")
         nc.vector.scalar_tensor_tensor(fg[:], f[:], lam[:], g[:], ALU.mult, ALU.mult, accum_out=alpha[:])
-        curve = wide("curve")
-        nc.vector.scalar_tensor_tensor(curve[:], f[:], kappa[:], u[:], ALU.mult, ALU.mult)
+        nc.vector.scalar_tensor_tensor(curve[:, second], f[:, second], kappa[:], u[:, second], ALU.mult, ALU.mult)
         term_g = wide("term_g")
         nc.scalar.activation(term_g[:], g_lam[:], ACT.Copy, scale=sum_ff[:])
         term_f = wide("term_f")
-        nc.vector.scalar_tensor_tensor(term_f[:], curve[:], alpha[:], f[:], ALU.add, ALU.mult)
+        for h in halves:
+            nc.vector.scalar_tensor_tensor(term_f[:, h], curve[:, h], alpha[:], f[:, h], ALU.add, ALU.mult)
 
         nc.vector.tensor_tensor(placed[:].indirect(offsets[:]), term_f[:], term_g[:], ALU.add)
 

@@ -20,7 +20,7 @@ TOKENS = 2048
 SLOTS = 512
 ROWS = 128
 PENALTY = 2.0 * 512.0 * 512.0
-STORE_WIDTHS = (256, 512, 512, 512, 256)
+STORE_WIDTHS = (128, 384, 512, 512, 512)
 
 FLOPS = 3 * 2 * 512 * ROWS * SLOTS
 
@@ -40,59 +40,50 @@ def tile_attend_gpeitherquestion_kernel(tc, query, query2, keys_words, keys_scal
 
         offsets = pool.tile([P, SLOTS // 16], U16, name="offsets")
         nc.sync.dma_start(offsets[:], offs)
+
+        def load_scale_rows(scales, name, second_half):
+            rows = pool.tile([P, TOKENS], U8, name=name, tag=name)
+            nc.vector.memset(rows[:, :TOKENS // 2].bitcast(I32), 0)
+            second_half.memset(rows[:, TOKENS // 2:].bitcast(I32), 0)
+            for j in range(4):
+                nc.sync.dma_start(rows[j:P:32, :].bitcast(I32), scales[0, j:16:4, :].bitcast(I32))
+            return rows
+
+        def load_words(words, name):
+            table = pool.tile([P, TOKENS], U16, name=name)
+            nc.sync.dma_start(table[:].bitcast(I32), words[0].bitcast(I32))
+            return table
+
+        def load_rows(rows, name):
+            raw = pool.tile([P, PACK, ROWS], F32, name=name, tag=name, align_bytes=64)
+            nc.sync.dma_start(raw[:], rows.rearrange("(p t) q -> p t q", t=PACK))
+            return raw
+
+        key_table = load_words(keys_words, "key_table")
+        key_rows = load_scale_rows(keys_scales, "key_rows", nc.gpsimd)
+        raw_b = load_rows(query2, "raw_b")
+        raw_a = load_rows(query, "raw_a")
+        val_table = load_words(vals_words, "val_table")
+        raw_c = load_rows(gout, "raw_c")
         size4 = pool.tile([P, PACK], F32, name="size4")
         nc.sync.dma_start(size4[:], size.rearrange("o (p c) -> (o p) c", c=PACK))
         th_sb = column("th_sb")
         nc.sync.dma_start(th_sb[:], th)
+        val_rows = load_scale_rows(vals_scales, "val_rows", nc.vector)
         gq_sb = column("gq_sb")
         nc.sync.dma_start(gq_sb[:], gq1)
-
-        def load_scale_rows(scales, name):
-            rows = pool.tile([P, TOKENS], U8, name=name)
-            nc.vector.memset(rows[:, :TOKENS // 2].bitcast(I32), 0)
-            nc.gpsimd.memset(rows[:, TOKENS // 2:].bitcast(I32), 0)
-            nc.sync.dma_start(rows[0:P:8, :].bitcast(I32), scales[0].bitcast(I32))
-            return rows
-
-        def load_words(words, name):
-            table = pool.tile([P, TOKENS], U16, name=name, tag=name)
-            nc.sync.dma_start(table[:].bitcast(I32), words[0].bitcast(I32))
-            return table
-
-        def load_rows(rows, name, tag):
-            raw = pool.tile([P, PACK, ROWS], F32, name=name, tag=tag, align_bytes=64)
-            nc.sync.dma_start(raw[:], rows.rearrange("(p t) q -> p t q", t=PACK))
-            return raw
-
-        key_rows = load_scale_rows(keys_scales, "key_rows")
-        val_rows = load_scale_rows(vals_scales, "val_rows")
-        key_table = load_words(keys_words, "key_table")
-        raw_b = load_rows(query2, "raw_b", "raw_b")
-        raw_a = load_rows(query, "raw_a", "stage")
-        val_table = load_words(vals_words, "val_table")
-        raw_c = load_rows(gout, "raw_c", "raw_c")
-
-        def zeroed_plane(name):
-            plane = pool.tile([P, SLOTS], U8, name=name, align_bytes=64)
-            nc.vector.memset(plane[:].bitcast(I32), 0)
-            return plane
-
-        key_plane = zeroed_plane("key_plane")
-        val_plane = zeroed_plane("val_plane")
+        base_sb = pool.tile([P, TOKENS], F32, name="base_sb")
+        nc.sync.dma_start(base_sb[:], base)
 
         identity = pool.tile([P, P], F32, name="identity")
         make_identity(nc, identity[:])
         half_th = column("half_th")
-        nc.scalar.activation(half_th[:], th_sb[:], ACT.Copy, scale=0.5)
+        nc.gpsimd.tensor_scalar(half_th[:], th_sb[:], 0.5, 0.0, ALU.mult, ALU.add)
         gq_k = column("gq_k")
-        nc.scalar.activation(gq_k[:], gq_sb[:], ACT.Copy, scale=PENALTY / 16.0)
-
-        size_bank = psum.tile([P, PACK, P], F32, name="size_bank")
-        for c in range(PACK):
-            nc.tensor.transpose(size_bank[:, c, :], size4[:, c:c + 1].to_broadcast([P, P]), identity[:])
+        nc.gpsimd.tensor_scalar(gq_k[:], gq_sb[:], PENALTY / 16.0, 0.0, ALU.mult, ALU.add)
 
         def interleave(raw, name):
-            grouped = pool.tile([P, ROWS, PACK], BF16, name=name, tag=name, align_bytes=64)
+            grouped = pool.tile([P, ROWS, PACK], BF16, name=name, align_bytes=64)
             nc.scalar.activation(grouped[:], raw[:].rearrange("p t q -> p q t"), ACT.Copy)
             return grouped
 
@@ -108,19 +99,14 @@ def tile_attend_gpeitherquestion_kernel(tc, query, query2, keys_words, keys_scal
             nc.vector.tensor_copy(picked[:], table[:].indirect(offsets[:]))
             return picked
 
-        def move_rows(queue, picked, plane):
-            for j in range(4):
-                queue.dma_start(plane[j:P:32, :].bitcast(I32), picked[8 * j:P:32, :].bitcast(I32))
-
         def product(stationary, words, plane, name):
             bank = psum.tile([P, SLOTS], F32, name=name)
             nc.tensor.matmul_mx(out=bank[:], lhsT=stationary[0][:].bitcast(FP8X4), lhsT_scale=stationary[1][:],
                                 rhs=words[:].bitcast(FP4X4), rhs_scale=plane[:], start=True, stop=True)
             return bank
 
-        key_bytes = gather(key_rows, U8, "key_bytes", "key_bytes")
-        move_rows(nc.scalar, key_bytes, key_plane)
         key_words = gather(key_table, U16, "key_words", "key_words")
+        key_plane = gather(key_rows, U8, "key_plane", "key_plane")
         grouped_b = interleave(raw_b, "grouped_b")
         grouped_a = interleave(raw_a, "grouped_a")
         quant_b = quantize(grouped_b, "qb")
@@ -128,32 +114,34 @@ def tile_attend_gpeitherquestion_kernel(tc, query, query2, keys_words, keys_scal
         score_b = product(quant_b, key_words, key_plane, "score_b")
         score_a = product(quant_a, key_words, key_plane, "score_a")
 
-        val_bytes = gather(val_rows, U8, "val_bytes", "stage")
-        move_rows(nc.sync, val_bytes, val_plane)
-        base_sb = pool.tile([P, TOKENS], F32, name="base_sb", tag="stage", align_bytes=64)
-        nc.sync.dma_start(base_sb[:], base)
+        size_bank = psum.tile([P, PACK, P], F32, name="size_bank")
+        for c in range(PACK):
+            nc.tensor.transpose(size_bank[:, c, :], size4[:, c:c + 1].to_broadcast([P, P]), identity[:])
+
         grouped_c = interleave(raw_c, "grouped_c")
-        val_words = gather(val_table, U16, "val_words", "val_words")
+        val_words = gather(val_table, U16, "val_words", "raw_a")
+        val_plane = gather(val_rows, U8, "val_plane", "val_plane")
         quant_c = quantize(grouped_c, "qc")
-        placed = pool.tile([P, TOKENS], F32, name="placed", tag="grouped_c", align_bytes=64)
-        nc.gpsimd.memset(placed[:], 0.0)
         c0 = product(quant_c, val_words, val_plane, "c0")
 
-        size_row = pool.tile([P, SLOTS], F32, name="size_row", tag="grouped_b", align_bytes=64)
-        nc.scalar.activation(size_row[:].rearrange("p (n c) -> p n c", c=PACK),
-                             size_bank[:].rearrange("p c n -> p n c"), ACT.Copy)
-
-        tb = wide("tb")
+        tb = pool.tile([P, SLOTS], F32, name="tb", tag="raw_c", align_bytes=64)
         nc.scalar.activation(tb[:], score_b[:], ACT.Tanh, bias=half_th[:], scale=-0.5)
         u = wide("u")
         nc.scalar.activation(u[:], score_a[:], ACT.Tanh, bias=half_th[:], scale=-0.5)
-        v = wide("v")
+        v = pool.tile([P, SLOTS], F32, name="v", tag="v")
         nc.scalar.activation(v[:], tb[:], ACT.Copy, bias=0.5, scale=0.5)
 
+        size_row = wide("size_row")
+        nc.scalar.activation(size_row[:].rearrange("p (n c) -> p n c", c=PACK),
+                             size_bank[:].rearrange("p c n -> p n c"), ACT.Copy)
+
         halves = (slice(0, SLOTS // 2), slice(SLOTS // 2, SLOTS))
-        m2 = pool.tile([P, SLOTS], F32, name="m2", tag="val_table")
+        m2 = pool.tile([P, SLOTS], F32, name="m2", tag="val_rows")
         for h in halves:
             nc.vector.scalar_tensor_tensor(m2[:, h], u[:, h], 1.0, v[:, h], ALU.add, ALU.mult)
+        placed = pool.tile([P, TOKENS], F32, name="placed", tag="v")
+        nc.gpsimd.memset(placed[:, :TOKENS // 2], 0.0)
+        nc.gpsimd.memset(placed[:, TOKENS // 2:], 0.0)
         p = wide("p")
         z = column("z")
         nc.scalar.activation(p[:], m2[:], ACT.Copy, bias=1.0, scale=-0.5, accum_out=z[:])

from contextlib import ExitStack

import concourse.mybir as mybir
from concourse.masks import make_identity

F32 = mybir.dt.float32
BF16 = mybir.dt.bfloat16
I32 = mybir.dt.int32
U32 = mybir.dt.uint32
U16 = mybir.dt.uint16
U8 = mybir.dt.uint8
FP8X4 = mybir.dt.float8_e4m3fn_x4
FP4X4 = mybir.dt.float4_e2m1fn_x4
ALU = mybir.AluOpType
ACT = mybir.ActivationFunctionType

P = 128
PACK = 4
TOKENS = 2048
SLOTS = 512
ROWS = 128
PENALTY = 2.0 * 512.0 * 512.0
STORE_WIDTHS = (128, 384, 512, 512, 512)

FLOPS = 3 * 2 * 512 * ROWS * SLOTS


def tile_attend_gpeitherquestion_kernel(tc, query, query2, keys_words, keys_scales, th, gout, vals_words,
                                         vals_scales, size, base, gq1, offs, out):
    nc = tc.nc
    with ExitStack() as ctx:
        pool = ctx.enter_context(tc.tile_pool(name="held", bufs=1))
        psum = ctx.enter_context(tc.psum_pool(name="psum", bufs=1))

        def wide(name):
            return pool.tile([P, SLOTS], F32, name=name)

        def column(name):
            return pool.tile([P, 1], F32, name=name)

        offsets = pool.tile([P, SLOTS // 16], U16, name="offsets")
        nc.sync.dma_start(offsets[:], offs)

        def load_scale_rows(scales, name, second_half):
            rows = pool.tile([P, TOKENS], U8, name=name, tag=name)
            nc.vector.memset(rows[:, :TOKENS // 2].bitcast(I32), 0)
            second_half.memset(rows[:, TOKENS // 2:].bitcast(I32), 0)
            for j in range(4):
                nc.sync.dma_start(rows[j:P:32, :].bitcast(I32), scales[0, j:16:4, :].bitcast(I32))
            return rows

        def load_words(words, name):
            table = pool.tile([P, TOKENS], U16, name=name)
            nc.sync.dma_start(table[:].bitcast(I32), words[0].bitcast(I32))
            return table

        def load_rows(rows, name):
            raw = pool.tile([P, PACK, ROWS], F32, name=name, tag=name, align_bytes=64)
            nc.sync.dma_start(raw[:], rows.rearrange("(p t) q -> p t q", t=PACK))
            return raw

        key_table = load_words(keys_words, "key_table")
        key_rows = load_scale_rows(keys_scales, "key_rows", nc.gpsimd)
        raw_b = load_rows(query2, "raw_b")
        raw_a = load_rows(query, "raw_a")
        val_table = load_words(vals_words, "val_table")
        raw_c = load_rows(gout, "raw_c")
        size4 = pool.tile([P, PACK], F32, name="size4")
        nc.sync.dma_start(size4[:], size.rearrange("o (p c) -> (o p) c", c=PACK))
        th_sb = column("th_sb")
        nc.sync.dma_start(th_sb[:], th)
        val_rows = load_scale_rows(vals_scales, "val_rows", nc.vector)
        gq_sb = column("gq_sb")
        nc.sync.dma_start(gq_sb[:], gq1)
        base_sb = pool.tile([P, TOKENS], F32, name="base_sb")
        nc.sync.dma_start(base_sb[:], base)

        identity = pool.tile([P, P], F32, name="identity")
        make_identity(nc, identity[:])
        half_th = column("half_th")
        nc.gpsimd.tensor_scalar(half_th[:], th_sb[:], 0.5, 0.0, ALU.mult, ALU.add)
        gq_k = column("gq_k")
        nc.gpsimd.tensor_scalar(gq_k[:], gq_sb[:], PENALTY / 16.0, 0.0, ALU.mult, ALU.add)

        def interleave(raw, name):
            grouped = pool.tile([P, ROWS, PACK], BF16, name=name, align_bytes=64)
            nc.scalar.activation(grouped[:], raw[:].rearrange("p t q -> p q t"), ACT.Copy)
            return grouped

        def quantize(grouped, name):
            codes = pool.tile([P, ROWS], U32, name=name + "_codes", align_bytes=64)
            plane = pool.tile([P, ROWS], U8, name=name + "_plane", align_bytes=64)
            nc.vector.quantize_mx(out=codes[:].bitcast(FP8X4), scales=plane[:],
                                  in_=grouped[:].rearrange("p q t -> p (q t)"))
            return codes, plane

        def gather(table, dtype, name, tag):
            picked = pool.tile([P, SLOTS], dtype, name=name, tag=tag, align_bytes=64)
            nc.vector.tensor_copy(picked[:], table[:].indirect(offsets[:]))
            return picked

        def product(stationary, words, plane, name):
            bank = psum.tile([P, SLOTS], F32, name=name)
            nc.tensor.matmul_mx(out=bank[:], lhsT=stationary[0][:].bitcast(FP8X4), lhsT_scale=stationary[1][:],
                                rhs=words[:].bitcast(FP4X4), rhs_scale=plane[:], start=True, stop=True)
            return bank

        key_words = gather(key_table, U16, "key_words", "key_words")
        key_plane = gather(key_rows, U8, "key_plane", "key_plane")
        grouped_b = interleave(raw_b, "grouped_b")
        grouped_a = interleave(raw_a, "grouped_a")
        quant_b = quantize(grouped_b, "qb")
        quant_a = quantize(grouped_a, "qa")
        score_b = product(quant_b, key_words, key_plane, "score_b")
        score_a = product(quant_a, key_words, key_plane, "score_a")

        size_bank = psum.tile([P, PACK, P], F32, name="size_bank")
        for c in range(PACK):
            nc.tensor.transpose(size_bank[:, c, :], size4[:, c:c + 1].to_broadcast([P, P]), identity[:])

        grouped_c = interleave(raw_c, "grouped_c")
        val_words = gather(val_table, U16, "val_words", "raw_a")
        val_plane = gather(val_rows, U8, "val_plane", "val_plane")
        quant_c = quantize(grouped_c, "qc")
        c0 = product(quant_c, val_words, val_plane, "c0")

        tb = pool.tile([P, SLOTS], F32, name="tb", tag="raw_c", align_bytes=64)
        nc.scalar.activation(tb[:], score_b[:], ACT.Tanh, bias=half_th[:], scale=-0.5)
        u = wide("u")
        nc.scalar.activation(u[:], score_a[:], ACT.Tanh, bias=half_th[:], scale=-0.5)
        v = pool.tile([P, SLOTS], F32, name="v", tag="v")
        nc.scalar.activation(v[:], tb[:], ACT.Copy, bias=0.5, scale=0.5)

        size_row = wide("size_row")
        nc.scalar.activation(size_row[:].rearrange("p (n c) -> p n c", c=PACK),
                             size_bank[:].rearrange("p c n -> p n c"), ACT.Copy)

        halves = (slice(0, SLOTS // 2), slice(SLOTS // 2, SLOTS))
        m2 = pool.tile([P, SLOTS], F32, name="m2", tag="val_rows")
        for h in halves:
            nc.vector.scalar_tensor_tensor(m2[:, h], u[:, h], 1.0, v[:, h], ALU.add, ALU.mult)
        placed = pool.tile([P, TOKENS], F32, name="placed", tag="v")
        nc.gpsimd.memset(placed[:, :TOKENS // 2], 0.0)
        nc.gpsimd.memset(placed[:, TOKENS // 2:], 0.0)
        p = wide("p")
        z = column("z")
        nc.scalar.activation(p[:], m2[:], ACT.Copy, bias=1.0, scale=-0.5, accum_out=z[:])
        g = wide("g")
        for h in halves:
            nc.vector.scalar_tensor_tensor(g[:, h], u[:, h], 1.0, m2[:, h], ALU.subtract, ALU.mult)
        cs = wide("cs")
        nc.vector.tensor_tensor(cs[:], c0[:], size_row[:], ALU.mult)
        r = column("r")
        nc.vector.reciprocal(r[:], z[:])
        weighted = wide("weighted")
        mean = column("mean")
        nc.vector.scalar_tensor_tensor(weighted[:], cs[:], r[:], p[:], ALU.mult, ALU.mult, accum_out=mean[:])
        kappa = column("kappa")
        nc.vector.tensor_scalar(kappa[:], r[:], r[:], gq_k[:], ALU.mult, ALU.mult)
        lam = column("lam")
        nc.vector.tensor_scalar(lam[:], kappa[:], r[:], 0.25, ALU.mult, ALU.mult)
        g_lam = wide("g_lam")
        nc.scalar.activation(g_lam[:], g[:], ACT.Copy, scale=lam[:])
        f = wide("f")
        for h in halves:
            nc.vector.scalar_tensor_tensor(f[:, h], cs[:, h], mean[:], g[:, h], ALU.subtract, ALU.mult)
        f_sq = wide("f_sq")
        sum_ff = column("sum_ff")
        nc.scalar.activation(f_sq[:], f[:], ACT.Square, accum_out=sum_ff[:])
        curve = wide("curve")
        first, second = halves
        nc.vector.scalar_tensor_tensor(curve[:, first], f[:, first], kappa[:], u[:, first], ALU.mult, ALU.mult)
        fg = wide("fg")
        alpha = column("alpha")
        nc.vector.scalar_tensor_tensor(fg[:], f[:], lam[:], g[:], ALU.mult, ALU.mult, accum_out=alpha[:])
        nc.vector.scalar_tensor_tensor(curve[:, second], f[:, second], kappa[:], u[:, second], ALU.mult, ALU.mult)
        term_g = wide("term_g")
        nc.scalar.activation(term_g[:], g_lam[:], ACT.Copy, scale=sum_ff[:])
        term_f = wide("term_f")
        for h in halves:
            nc.vector.scalar_tensor_tensor(term_f[:, h], curve[:, h], alpha[:], f[:, h], ALU.add, ALU.mult)

        nc.vector.tensor_tensor(placed[:].indirect(offsets[:]), term_f[:], term_g[:], ALU.add)

        start = 0
        for n, width in enumerate(STORE_WIDTHS):
            cols = slice(start, start + width)
            result = pool.tile([P, width], F32, name="result%d" % n)
            nc.vector.tensor_tensor(result[:], placed[:, cols], base_sb[:, cols], ALU.add)
            queue = nc.sync if n % 2 == 0 else nc.scalar
            queue.dma_start(out[:, cols], result[:])
            start = start + width
